import numpy as np
import ml_dtypes


def mxq(x, axis, fmt="e4m3"):
    dtype, down = {"e4m3": (ml_dtypes.float8_e4m3fn, 7), "e5m2": (ml_dtypes.float8_e5m2, 14)}[fmt]
    v = np.moveaxis(np.asarray(x, np.float32).astype(ml_dtypes.bfloat16).astype(np.float64), axis, -1)
    blocks = v.reshape(v.shape[:-1] + (-1, 32))
    amax = np.abs(blocks).max(-1, keepdims=True)
    byte = np.maximum(np.where(amax > 0, np.frexp(amax)[1] - 1 + 127, 0) - down, 1)
    scale = np.exp2(byte - 127.0)
    codes = (blocks / scale).astype(np.float32).astype(dtype).astype(np.float64)
    return np.moveaxis((codes * scale).reshape(v.shape), -1, axis)


WIDE = False


def mx_kscale(k):
    if not WIDE:
        return np.ones(k)
    levels = np.array([10, -10, 5, -5, 0])
    if k % 512:
        return np.exp2(np.random.permutation(np.resize(levels, k // 32))).repeat(32)
    a = np.empty((k // 512, 16))
    for p in range(k // 512):
        a[p, :8] = np.random.permutation(np.resize(levels, 8))
        for g in range(8):
            far = levels[np.abs(levels - a[p, g]) >= 10]
            a[p, g + 8] = far[np.random.randint(len(far))]
    return np.exp2(a.ravel()).repeat(32)


def f64(x):
    return np.asarray(x).astype(np.float64)


def striped(idx):
    return np.tile(idx.reshape(-1, 16).T, (8, 1)).astype(np.uint16)


def unstriped(offs):
    return offs[:16].T.reshape(-1).astype(np.int64)


E2M1 = np.array([0.0, 0.5, 1.0, 1.5, 2.0, 3.0, 4.0, 6.0, -0.0, -0.5, -1.0, -1.5, -2.0, -3.0, -4.0, -6.0])


def pack_weight(w, fmt):
    k, n = w.shape
    w = f64(np.asarray(w, np.float32).astype(ml_dtypes.bfloat16)).reshape(k // 32, 32, n)
    amax = np.abs(w).max(1)
    if fmt == "e4m3":
        byte = np.frexp(amax)[1] - 1 + 127 - 7
    else:
        mant, ex = np.frexp(amax / 6.0)
        byte = np.where(mant > 0.5, ex, ex - 1) + 127
    byte = np.clip(np.where(amax > 0, byte, 1), 1, 254)
    scaled = (w * np.exp2(127.0 - byte)[:, None, :]).reshape(k, n).astype(np.float32)
    by_word = np.ascontiguousarray(scaled.reshape(k // 512, 128, 4, n).transpose(0, 1, 3, 2))
    if fmt == "e4m3":
        words = by_word.astype(ml_dtypes.float8_e4m3fn).view(np.uint8)
    else:
        c = by_word.astype(ml_dtypes.float4_e2m1fn).view(np.uint8) & 0xF
        words = (c[..., 0::2] | (c[..., 1::2] << 4)).reshape(k // 512, 128, 2 * n)
    return np.ascontiguousarray(words), np.ascontiguousarray(byte.astype(np.uint8).reshape(k // 512, 16, n))


def unpack_weight(words, scales, fmt):
    g, _, n = scales.shape
    words = np.ascontiguousarray(words).reshape(g, 128, n, -1)
    if fmt == "e4m3":
        vals = words.view(ml_dtypes.float8_e4m3fn).astype(np.float64)
    else:
        nib = np.empty((g, 128, n, 4), np.uint8)
        nib[..., 0::2] = words & 0xF
        nib[..., 1::2] = words >> 4
        vals = E2M1[nib]
    vals = vals * np.repeat(np.exp2(scales.astype(np.float64) - 127.0), 8, axis=1)[..., None]
    return vals.transpose(0, 1, 3, 2).reshape(g * 512, n)


def gelu(v):
    return 0.5 * v * (1.0 + np.tanh(np.sqrt(2.0 / np.pi) * (v + 0.044715 * v**3)))


K, T, E, C, H, N = 512, 768, 4, 256, 512, 128
PAD = 32


def by_expert(wq, xq):
    return np.concatenate([wq[e].T @ xq[:, e * C:(e + 1) * C] for e in range(E)], axis=1)


def setup_inputs():
    n = np.random.standard_normal
    s = mx_kscale(K)[:, None]
    u = mx_kscale(H)
    first = np.random.permutation(np.repeat(np.arange(E), T // E))
    second = (first + 1 + np.random.permutation(np.repeat(np.arange(E - 1), -(-T // (E - 1)))[:T])) % E
    while np.bincount(second, minlength=E).max() != T // E:
        load = np.bincount(second, minlength=E); hi, lo = int(load.argmax()), int(load.argmin())
        t = np.flatnonzero((second == hi) & (first != lo))[0]; second[t] = lo
    slot_token = np.empty(E * C, np.int64); pos = np.empty((2, T), np.int64); fill = np.zeros(E, np.int64)
    place = np.stack([np.random.permutation(C) for _ in range(E)])
    for r, deal in enumerate((first, second)):
        for t in np.random.permutation(T):
            e = deal[t]
            if fill[e] < C: j = e * C + place[e, fill[e]]; fill[e] += 1; slot_token[j] = t; pos[r, t] = j
            else: pos[r, t] = E * C + t % PAD
    g = np.random.uniform(0.2, 0.8, T)
    w1 = [pack_weight(m, "e2m1") for m in n((E, K, H)) / np.sqrt(K) / s[None] * u[None, None, :]]
    w2 = [pack_weight(m, "e2m1") for m in n((E, H, N)) / np.sqrt(H) / u[None, :, None]]
    return {
        "xT": (n((K, T)) * s).astype(np.float32),
        "w1_words": np.stack([m[0] for m in w1]),
        "w1_scales": np.stack([m[1] for m in w1]),
        "w2_words": np.stack([m[0] for m in w2]),
        "w2_scales": np.stack([m[1] for m in w2]),
        "gate": np.stack([np.tile(g, (N, 1)), np.tile(1.0 - g, (N, 1))]).astype(np.float32),
        "offs": striped(slot_token),
        "pos1": striped(pos[0]),
        "pos2": striped(pos[1]),
    }


def reference(xT, w1_words, w1_scales, w2_words, w2_scales, gate, offs, pos1, pos2):
    idx = unstriped(offs)
    w1 = np.stack([unpack_weight(w1_words[e], w1_scales[e], "e2m1") for e in range(E)])
    w2 = np.stack([unpack_weight(w2_words[e], w2_scales[e], "e2m1") for e in range(E)])
    xq = mxq(f64(xT)[:, idx], 0, "e4m3")
    h = gelu(by_expert(w1, xq))
    y = by_expert(w2, mxq(h, 0, "e4m3"))
    y = np.concatenate([y, np.zeros((N, PAD))], axis=1)
    return f64(gate[0]) * y[:, unstriped(pos1)] + f64(gate[1]) * y[:, unstriped(pos2)]

@@ -1,0 +1,191 @@
+from contextlib import ExitStack
+
+import concourse.mybir as mybir
+
+K, T, E, C, H, N = 512, 768, 4, 256, 512, 128
+PAD = 32
+S = E * C
+P = 128
+U = 128
+
+F32 = mybir.dt.float32
+BF16 = mybir.dt.bfloat16
+I32 = mybir.dt.int32
+U32 = mybir.dt.uint32
+U16 = mybir.dt.uint16
+U8 = mybir.dt.uint8
+FP8X4 = mybir.dt.float8_e4m3fn_x4
+FP4X4 = mybir.dt.float4_e2m1fn_x4
+ACT = mybir.ActivationFunctionType
+ALU = mybir.AluOpType
+
+FLOPS = 2 * S * (K * H + H * N)
+
+
+def tile_moe_cap2_mlp_gelu_kernel(tc, xT, w1_words, w1_scales, w2_words, w2_scales, gate, offs, pos1, pos2, out):
+    nc = tc.nc
+    with ExitStack() as ctx:
+        keep = ctx.enter_context(tc.tile_pool(name="keep", bufs=1))
+        apsum = ctx.enter_context(tc.psum_pool(name="apsum", bufs=6))
+        ypsum = ctx.enter_context(tc.psum_pool(name="ypsum", bufs=1))
+
+        offs_sb = keep.tile([P, S // 16], U16, name="offs_sb")
+        pos1_sb = keep.tile([P, T // 16], U16, name="pos1_sb")
+        pos2_sb = keep.tile([P, T // 16], U16, name="pos2_sb")
+        x_raw = keep.tile([P, 4, T], F32, name="x_raw")
+        x_bf = keep.tile([P, T, 4], BF16, name="x_bf", align_bytes=64)
+        x_codes = keep.tile([P, T], U32, name="x_codes", align_bytes=64)
+        x_scales = keep.tile([P, T], U8, name="x_scales", align_bytes=64)
+        w1_raw = keep.tile([P, E, 2 * H], U8, name="w1_raw", align_bytes=64)
+        w1_perm = keep.tile([P, E, 2 * H], U8, name="w1_perm", align_bytes=64)
+        s1_raw = keep.tile([P, E, H], U8, name="s1_raw", align_bytes=64)
+        s1_perm = keep.tile([P, E, H], U8, name="s1_perm", align_bytes=64)
+        w2_sb = keep.tile([P, E, 2 * N], U8, name="w2_sb", align_bytes=64)
+        s2_sb = keep.tile([P, E, N], U8, name="s2_sb", align_bytes=64)
+        gate_sb = keep.tile([P, 2, T], F32, name="gate_sb")
+        y_sb = keep.tile([P, S + PAD], F32, name="y_sb")
+        t1 = keep.tile([P, T], F32, name="t1")
+        t2 = keep.tile([P, T], F32, name="t2")
+        o_sb = keep.tile([P, T], F32, name="o_sb")
+        dummy = keep.tile([P, 1], F32, name="dummy")
+        dummy2 = keep.tile([P, 1], F32, name="dummy2")
+
+        nc.vector.memset(s1_raw[:].rearrange("p e h -> p (e h)").bitcast(I32), 0)
+        nc.vector.memset(dummy[:], 0.0)
+        nc.vector.memset(x_scales[:].bitcast(I32), 0)
+        nc.vector.memset(s2_sb[:].rearrange("p e h -> p (e h)").bitcast(I32), 0)
+        nc.vector.memset(y_sb[:, S : S + PAD], 0.0)
+
+        x_view = xT.rearrange("(p j) t -> p j t", j=4)
+        s1_i32 = w1_scales.rearrange("e s q h -> q (e s) h").bitcast(I32)
+        s2_i32 = w2_scales.rearrange("e s q h -> q (e s) h").bitcast(I32)
+        for q in range(4):
+            nc.scalar.dma_start(out=s1_raw[32 * q : 32 * q + 4, :, :].bitcast(I32), in_=s1_i32[4 * q : 4 * q + 4, :, :])
+        nc.scalar.activation(out=dummy2[:], in_=dummy[:], func=ACT.Gelu_apprx_tanh)
+
+        w1_i32 = w1_words.rearrange("e s p b -> p (e s) b").bitcast(I32)
+        nc.sync.dma_start(out=w1_raw[:, 0:1, :].bitcast(I32), in_=w1_i32[:, 0:1, :])
+        nc.sync.dma_start(out=w1_raw[:, 1:E, :].bitcast(I32), in_=w1_i32[:, 1:E, :])
+        for lo in range(0, T, 256):
+            nc.sync.dma_start(out=x_raw[:, :, lo : lo + 256], in_=x_view[:, :, lo : lo + 256])
+        nc.sync.dma_start(offs_sb[:], offs)
+        nc.sync.dma_start(out=w2_sb[:].bitcast(I32), in_=w2_words.rearrange("e s p b -> p (e s) b").bitcast(I32))
+        for q in range(4):
+            nc.sync.dma_start(out=s2_sb[32 * q : 32 * q + 4, :, :].bitcast(I32), in_=s2_i32[4 * q : 4 * q + 4, :, :])
+        nc.sync.dma_start(pos1_sb[:], pos1)
+        nc.sync.dma_start(pos2_sb[:], pos2)
+        for r in range(2):
+            nc.sync.dma_start(out=gate_sb[:, r, :], in_=gate[r])
+
+        def permute(e):
+            nc.vector.tensor_copy(
+                out=w1_perm[:, e, :].bitcast(U16).rearrange("p (t m) -> p t m", t=4),
+                in_=w1_raw[:, e, :].bitcast(U16).rearrange("p (m t) -> p t m", t=4),
+            )
+            nc.vector.tensor_copy(
+                out=s1_perm[:, e, :].rearrange("p (t m) -> p t m", t=4),
+                in_=s1_raw[:, e, :].rearrange("p (m t) -> p t m", t=4),
+            )
+
+        def cast(engine, lo, hi):
+            dst = x_bf[:, lo:hi, :]
+            src = x_raw[:, :, lo:hi].rearrange("p j t -> p t j")
+            if engine == "scalar":
+                nc.scalar.copy(out=dst, in_=src)
+            else:
+                nc.vector.tensor_copy(out=dst, in_=src)
+
+        def quantize_x(lo, hi):
+            nc.vector.quantize_mx(
+                out=x_codes[:, lo:hi].bitcast(FP8X4),
+                scales=x_scales[:, lo:hi],
+                in_=x_bf[:, lo:hi, :].rearrange("p t j -> p (t j)"),
+            )
+
+        permute(0)
+        cast("scalar", 0, 256)
+        cast("scalar", 256, 512)
+        quantize_x(0, 256)
+        cast("vector", 512, 768)
+        quantize_x(256, 768)
+
+        g_codes = [keep.tile([P, C], U32, name="g_codes%d" % e, align_bytes=64) for e in range(E)]
+        g_scales = [keep.tile([P, C], U8, name="g_scales%d" % e, align_bytes=64) for e in range(E)]
+
+        def gather(e):
+            lst = offs_sb[:, e * (C // 16) : (e + 1) * (C // 16)]
+            nc.vector.tensor_copy(g_codes[e][:], x_codes[:].indirect(lst))
+            nc.vector.tensor_copy(g_scales[e][:], x_scales[:].indirect(lst))
+
+        y_banks = [ypsum.tile([P, 2 * C], F32, name="y_bank%d" % b) for b in range(2)]
+
+        h = [keep.tile([P, C, 4], BF16, name="h%d" % e, align_bytes=64) for e in range(E)]
+        h_codes = [keep.tile([P, C], U32, name="h_codes%d" % e, align_bytes=64) for e in range(E)]
+        h_scales = [keep.tile([P, C], U8, name="h_scales%d" % e, align_bytes=64) for e in range(E)]
+
+        def first_layer(e):
+            for u in range(2):
+                bank = apsum.tile([P, 4 * U], F32, name="bank")
+                cols = slice(u * U, (u + 1) * U)
+                for t in range(4):
+                    nc.tensor.matmul_mx(
+                        out=bank[:, t * U : (t + 1) * U],
+                        lhsT=w1_perm[:, e, t * 256 : (t + 1) * 256].bitcast(FP4X4),
+                        lhsT_scale=s1_perm[:, e, t * 128 : (t + 1) * 128],
+                        rhs=g_codes[e][:, cols].bitcast(FP8X4),
+                        rhs_scale=g_scales[e][:, cols],
+                        start=True,
+                        stop=True,
+                    )
+                nc.scalar.activation(out=h[e][:, cols, :], in_=bank[:].rearrange("p (t c) -> p c t", t=4), func=ACT.Gelu_apprx_tanh)
+
+        def second_layer(e, lo, hi):
+            nc.vector.quantize_mx(
+                out=h_codes[e][:, lo:hi].bitcast(FP8X4),
+                scales=h_scales[e][:, lo:hi],
+                in_=h[e][:, lo:hi, :].rearrange("p c t -> p (c t)"),
+            )
+            base = (e % 2) * C
+            nc.tensor.matmul_mx(
+                out=y_banks[e // 2][:, base + lo : base + hi],
+                lhsT=w2_sb[:, e, :].bitcast(FP4X4),
+                lhsT_scale=s2_sb[:, e, :],
+                rhs=h_codes[e][:, lo:hi].bitcast(FP8X4),
+                rhs_scale=h_scales[e][:, lo:hi],
+                start=True,
+                stop=True,
+            )
+
+        gather(0)
+        first_layer(0)
+        permute(1)
+        gather(1)
+        first_layer(1)
+        permute(2)
+        gather(2)
+        first_layer(2)
+        second_layer(0, 0, C)
+        permute(3)
+        gather(3)
+        first_layer(3)
+        second_layer(1, 0, C)
+        nc.scalar.copy(out=y_sb[:, 0 : 2 * C], in_=y_banks[0][:])
+        second_layer(2, 0, C)
+        nc.vector.tensor_copy(out=y_sb[:, 2 * C : 3 * C], in_=y_banks[1][:, 0:C])
+        second_layer(3, 0, U)
+        second_layer(3, U, C)
+        nc.vector.tensor_copy(out=y_sb[:, 3 * C : 4 * C], in_=y_banks[1][:, C : 2 * C])
+
+        def pick(lo, hi, p_sb, r, t):
+            nc.vector.tensor_tensor(t[:, lo:hi], y_sb[:].indirect(p_sb[:, lo // 16 : hi // 16]), gate_sb[:, r, lo:hi], ALU.mult)
+
+        def finish(lo, hi):
+            nc.vector.tensor_add(o_sb[:, lo:hi], t1[:, lo:hi], t2[:, lo:hi])
+            nc.sync.dma_start(out=out[:, lo:hi], in_=o_sb[:, lo:hi])
+
+        pick(0, 512, pos1_sb, 0, t1)
+        pick(0, 512, pos2_sb, 1, t2)
+        pick(512, 768, pos1_sb, 0, t1)
+        finish(0, 512)
+        pick(512, 768, pos2_sb, 1, t2)
+        finish(512, 768)

@@ -1,6 +1,7 @@
 from contextlib import ExitStack
 
 import concourse.mybir as mybir
+from concourse.masks import make_identity
 
 K, T, E, C, H, N = 512, 768, 4, 256, 512, 128
 PAD = 32
@@ -26,7 +27,8 @@ def tile_moe_cap2_mlp_gelu_kernel(tc, xT, w1_words, w1_scales, w2_words, w2_scal
     nc = tc.nc
     with ExitStack() as ctx:
         keep = ctx.enter_context(tc.tile_pool(name="keep", bufs=1))
-        apsum = ctx.enter_context(tc.psum_pool(name="apsum", bufs=6))
+        apsum = ctx.enter_context(tc.psum_pool(name="apsum", bufs=4))
+        xpsum = ctx.enter_context(tc.psum_pool(name="xpsum", bufs=2))
         ypsum = ctx.enter_context(tc.psum_pool(name="ypsum", bufs=1))
 
         offs_sb = keep.tile([P, S // 16], U16, name="offs_sb")
@@ -50,6 +52,7 @@ def tile_moe_cap2_mlp_gelu_kernel(tc, xT, w1_words, w1_scales, w2_words, w2_scal
         dummy = keep.tile([P, 1], F32, name="dummy")
         dummy2 = keep.tile([P, 1], F32, name="dummy2")
 
+        ident = keep.tile([P, P], F32, name="ident")
         nc.vector.memset(s1_raw[:].rearrange("p e h -> p (e h)").bitcast(I32), 0)
         nc.vector.memset(dummy[:], 0.0)
         nc.vector.memset(x_scales[:].bitcast(I32), 0)
@@ -64,11 +67,12 @@ def tile_moe_cap2_mlp_gelu_kernel(tc, xT, w1_words, w1_scales, w2_words, w2_scal
         nc.scalar.activation(out=dummy2[:], in_=dummy[:], func=ACT.Gelu_apprx_tanh)
 
         w1_i32 = w1_words.rearrange("e s p b -> p (e s) b").bitcast(I32)
-        nc.sync.dma_start(out=w1_raw[:, 0:1, :].bitcast(I32), in_=w1_i32[:, 0:1, :])
-        nc.sync.dma_start(out=w1_raw[:, 1:E, :].bitcast(I32), in_=w1_i32[:, 1:E, :])
+        make_identity(nc, ident[:])
+        nc.sync.dma_start(out=w1_raw[:, 2:4, :].bitcast(I32), in_=w1_i32[:, 2:4, :])
         for lo in range(0, T, 256):
             nc.sync.dma_start(out=x_raw[:, :, lo : lo + 256], in_=x_view[:, :, lo : lo + 256])
         nc.sync.dma_start(offs_sb[:], offs)
+        nc.sync.dma_start(out=w1_raw[:, 0:2, :].bitcast(I32), in_=w1_i32[:, 0:2, :])
         nc.sync.dma_start(out=w2_sb[:].bitcast(I32), in_=w2_words.rearrange("e s p b -> p (e s) b").bitcast(I32))
         for q in range(4):
             nc.sync.dma_start(out=s2_sb[32 * q : 32 * q + 4, :, :].bitcast(I32), in_=s2_i32[4 * q : 4 * q + 4, :, :])
@@ -88,8 +92,8 @@ def tile_moe_cap2_mlp_gelu_kernel(tc, xT, w1_words, w1_scales, w2_words, w2_scal
             )
 
         def cast(engine, lo, hi):
-            dst = x_bf[:, lo:hi, :]
-            src = x_raw[:, :, lo:hi].rearrange("p j t -> p t j")
+            dst = x_bf[:, lo:hi, :].rearrange("p (c i) j -> p c j i", i=4)
+            src = x_raw[:, :, lo:hi].rearrange("p j (c i) -> p c j i", i=4)
             if engine == "scalar":
                 nc.scalar.copy(out=dst, in_=src)
             else:
@@ -102,20 +106,23 @@ def tile_moe_cap2_mlp_gelu_kernel(tc, xT, w1_words, w1_scales, w2_words, w2_scal
                 in_=x_bf[:, lo:hi, :].rearrange("p t j -> p (t j)"),
             )
 
-        permute(0)
+        permute(2)
+        permute(3)
         cast("scalar", 0, 256)
-        cast("scalar", 256, 512)
-        quantize_x(0, 256)
-        cast("vector", 512, 768)
-        quantize_x(256, 768)
+        cast("vector", 256, 416)
+        cast("scalar", 416, 512)
+        quantize_x(0, 512)
+        cast("vector", 512, 672)
+        cast("scalar", 672, 768)
+        quantize_x(512, 768)
 
         g_codes = [keep.tile([P, C], U32, name="g_codes%d" % e, align_bytes=64) for e in range(E)]
         g_scales = [keep.tile([P, C], U8, name="g_scales%d" % e, align_bytes=64) for e in range(E)]
 
-        def gather(e):
-            lst = offs_sb[:, e * (C // 16) : (e + 1) * (C // 16)]
-            nc.vector.tensor_copy(g_codes[e][:], x_codes[:].indirect(lst))
-            nc.vector.tensor_copy(g_scales[e][:], x_scales[:].indirect(lst))
+        def gather(e, lo, hi):
+            lst = offs_sb[:, (e * C + lo) // 16 : (e * C + hi) // 16]
+            nc.vector.tensor_copy(g_codes[e][:, lo:hi], x_codes[:].indirect(lst))
+            nc.vector.tensor_copy(g_scales[e][:, lo:hi], x_scales[:].indirect(lst))
 
         y_banks = [ypsum.tile([P, 2 * C], F32, name="y_bank%d" % b) for b in range(2)]
 
@@ -156,25 +163,58 @@ def tile_moe_cap2_mlp_gelu_kernel(tc, xT, w1_words, w1_scales, w2_words, w2_scal
                 stop=True,
             )
 
-        gather(0)
-        first_layer(0)
-        permute(1)
-        gather(1)
-        first_layer(1)
-        permute(2)
-        gather(2)
-        first_layer(2)
+        def first_layer_moving(e):
+            rows = []
+            for u in range(2):
+                bank = apsum.tile([P, 4 * U], F32, name="bank")
+                cols = slice(u * U, (u + 1) * U)
+                nc.tensor.matmul_mx(
+                    out=bank[:],
+                    lhsT=g_codes[e][:, cols].bitcast(FP8X4),
+                    lhsT_scale=g_scales[e][:, cols],
+                    rhs=w1_raw[:, e, :].bitcast(FP4X4),
+                    rhs_scale=s1_raw[:, e, :],
+                    start=True,
+                    stop=True,
+                )
+                h_rows = keep.tile([P, H], BF16, name="h_rows%d_%d" % (e, u), align_bytes=64)
+                nc.scalar.activation(out=h_rows[:], in_=bank[:], func=ACT.Gelu_apprx_tanh)
+                rows.append(h_rows)
+            return rows
+
+        def turn(e, u, h_rows, engine):
+            words = h_rows[:].bitcast(F32).rearrange("p (w v) -> p v w", v=2)
+            turned = xpsum.tile([P, 2, P], F32, name="turned")
+            for v in range(2):
+                nc.tensor.transpose(turned[:, v, :], words[:, v, :], ident[:])
+            dst = h[e][:, u * U : (u + 1) * U, :].rearrange("p c t -> p (c t)").bitcast(F32).rearrange("p (c v) -> p c v", v=2)
+            src = turned[:].rearrange("p v c -> p c v")
+            if engine == "scalar":
+                nc.scalar.copy(out=dst, in_=src)
+            else:
+                nc.vector.tensor_copy(out=dst, in_=src)
+
+        gather(0, 0, U)
+        gather(0, U, C)
+        rows0 = first_layer_moving(0)
+        gather(1, 0, C)
+        turn(0, 0, rows0[0], "vector")
+        rows1 = first_layer_moving(1)
+        turn(0, 1, rows0[1], "scalar")
+        gather(2, 0, C)
         second_layer(0, 0, C)
-        permute(3)
-        gather(3)
-        first_layer(3)
+        first_layer(2)
+        turn(1, 0, rows1[0], "vector")
+        turn(1, 1, rows1[1], "scalar")
+        gather(3, 0, C)
         second_layer(1, 0, C)
-        nc.scalar.copy(out=y_sb[:, 0 : 2 * C], in_=y_banks[0][:])
+        first_layer(3)
         second_layer(2, 0, C)
-        nc.vector.tensor_copy(out=y_sb[:, 2 * C : 3 * C], in_=y_banks[1][:, 0:C])
+        nc.scalar.copy(out=y_sb[:, 0 : 2 * C], in_=y_banks[0][:])
         second_layer(3, 0, U)
+        nc.vector.tensor_copy(out=y_sb[:, 2 * C : 3 * C + U], in_=y_banks[1][:, 0 : C + U])
         second_layer(3, U, C)
-        nc.vector.tensor_copy(out=y_sb[:, 3 * C : 4 * C], in_=y_banks[1][:, C : 2 * C])
+        nc.scalar.copy(out=y_sb[:, 3 * C + U : 4 * C], in_=y_banks[1][:, C + U : 2 * C])
 
         def pick(lo, hi, p_sb, r, t):
             nc.vector.tensor_tensor(t[:, lo:hi], y_sb[:].indirect(p_sb[:, lo // 16 : hi // 16]), gate_sb[:, r, lo:hi], ALU.mult)
@@ -183,9 +223,10 @@ def tile_moe_cap2_mlp_gelu_kernel(tc, xT, w1_words, w1_scales, w2_words, w2_scal
             nc.vector.tensor_add(o_sb[:, lo:hi], t1[:, lo:hi], t2[:, lo:hi])
             nc.sync.dma_start(out=out[:, lo:hi], in_=o_sb[:, lo:hi])
 
-        pick(0, 512, pos1_sb, 0, t1)
-        pick(0, 512, pos2_sb, 1, t2)
-        pick(512, 768, pos1_sb, 0, t1)
-        finish(0, 512)
-        pick(512, 768, pos2_sb, 1, t2)
-        finish(512, 768)
+        pick(0, 768, pos1_sb, 0, t1)
+        pick(0, 384, pos2_sb, 1, t2)
+        pick(384, 640, pos2_sb, 1, t2)
+        finish(0, 384)
+        pick(640, 768, pos2_sb, 1, t2)
+        finish(384, 640)
+        finish(640, 768)

@@ -1,7 +1,6 @@
 from contextlib import ExitStack
 
 import concourse.mybir as mybir
-from concourse.masks import make_identity
 
 K, T, E, C, H, N = 512, 768, 4, 256, 512, 128
 PAD = 32
@@ -27,8 +26,7 @@ def tile_moe_cap2_mlp_gelu_kernel(tc, xT, w1_words, w1_scales, w2_words, w2_scal
     nc = tc.nc
     with ExitStack() as ctx:
         keep = ctx.enter_context(tc.tile_pool(name="keep", bufs=1))
-        apsum = ctx.enter_context(tc.psum_pool(name="apsum", bufs=4))
-        xpsum = ctx.enter_context(tc.psum_pool(name="xpsum", bufs=2))
+        apsum = ctx.enter_context(tc.psum_pool(name="apsum", bufs=6))
         ypsum = ctx.enter_context(tc.psum_pool(name="ypsum", bufs=1))
 
         offs_sb = keep.tile([P, S // 16], U16, name="offs_sb")
@@ -40,8 +38,9 @@ def tile_moe_cap2_mlp_gelu_kernel(tc, xT, w1_words, w1_scales, w2_words, w2_scal
         x_scales = keep.tile([P, T], U8, name="x_scales", align_bytes=64)
         w1_raw = keep.tile([P, E, 2 * H], U8, name="w1_raw", align_bytes=64)
         w1_perm = keep.tile([P, E, 2 * H], U8, name="w1_perm", align_bytes=64)
-        s1_raw = keep.tile([P, E, H], U8, name="s1_raw", align_bytes=64)
-        s1_perm = keep.tile([P, E, H], U8, name="s1_perm", align_bytes=64)
+        s1_raw = keep.tile([P, H], U8, name="s1_raw", align_bytes=64)
+        s1_perm = keep.tile([P, H], U8, name="s1_perm", align_bytes=64)
+        s1_planes = [s1_perm] + [keep.tile([P, H], U8, name="s1_plane%d" % e, align_bytes=64) for e in range(1, E)]
         w2_sb = keep.tile([P, E, 2 * N], U8, name="w2_sb", align_bytes=64)
         s2_sb = keep.tile([P, E, N], U8, name="s2_sb", align_bytes=64)
         gate_sb = keep.tile([P, 2, T], F32, name="gate_sb")
@@ -52,27 +51,33 @@ def tile_moe_cap2_mlp_gelu_kernel(tc, xT, w1_words, w1_scales, w2_words, w2_scal
         dummy = keep.tile([P, 1], F32, name="dummy")
         dummy2 = keep.tile([P, 1], F32, name="dummy2")
 
-        ident = keep.tile([P, P], F32, name="ident")
-        nc.vector.memset(s1_raw[:].rearrange("p e h -> p (e h)").bitcast(I32), 0)
+        nc.vector.memset(s1_raw[:].bitcast(I32), 0)
         nc.vector.memset(dummy[:], 0.0)
         nc.vector.memset(x_scales[:].bitcast(I32), 0)
         nc.vector.memset(s2_sb[:].rearrange("p e h -> p (e h)").bitcast(I32), 0)
         nc.vector.memset(y_sb[:, S : S + PAD], 0.0)
 
         x_view = xT.rearrange("(p j) t -> p j t", j=4)
-        s1_i32 = w1_scales.rearrange("e s q h -> q (e s) h").bitcast(I32)
+        s1_i32 = w1_scales.rearrange("e s q h -> (e s) q h").bitcast(I32)
         s2_i32 = w2_scales.rearrange("e s q h -> q (e s) h").bitcast(I32)
         for q in range(4):
-            nc.scalar.dma_start(out=s1_raw[32 * q : 32 * q + 4, :, :].bitcast(I32), in_=s1_i32[4 * q : 4 * q + 4, :, :])
+            nc.sync.dma_start(out=s1_raw[32 * q : 32 * q + 16, :].bitcast(I32), in_=s1_i32[:, 4 * q : 4 * q + 4, :])
         nc.scalar.activation(out=dummy2[:], in_=dummy[:], func=ACT.Gelu_apprx_tanh)
 
         w1_i32 = w1_words.rearrange("e s p b -> p (e s) b").bitcast(I32)
-        make_identity(nc, ident[:])
-        nc.sync.dma_start(out=w1_raw[:, 2:4, :].bitcast(I32), in_=w1_i32[:, 2:4, :])
+        for lo in range(0, E, 2):
+            nc.sync.dma_start(out=w1_raw[:, lo : lo + 2, :].bitcast(I32), in_=w1_i32[:, lo : lo + 2, :])
         for lo in range(0, T, 256):
             nc.sync.dma_start(out=x_raw[:, :, lo : lo + 256], in_=x_view[:, :, lo : lo + 256])
         nc.sync.dma_start(offs_sb[:], offs)
-        nc.sync.dma_start(out=w1_raw[:, 0:2, :].bitcast(I32), in_=w1_i32[:, 0:2, :])
+
+        nc.vector.tensor_copy(
+            out=s1_perm[:].rearrange("p (t m) -> p t m", t=4),
+            in_=s1_raw[:].rearrange("p (m t) -> p t m", t=4),
+        )
+        for e in range(1, E):
+            rows = P - 4 * e
+            nc.sync.dma_start(out=s1_planes[e][0:rows, :].bitcast(I32), in_=s1_perm[4 * e : P, :].bitcast(I32))
         nc.sync.dma_start(out=w2_sb[:].bitcast(I32), in_=w2_words.rearrange("e s p b -> p (e s) b").bitcast(I32))
         for q in range(4):
             nc.sync.dma_start(out=s2_sb[32 * q : 32 * q + 4, :, :].bitcast(I32), in_=s2_i32[4 * q : 4 * q + 4, :, :])
@@ -81,14 +86,10 @@ def tile_moe_cap2_mlp_gelu_kernel(tc, xT, w1_words, w1_scales, w2_words, w2_scal
         for r in range(2):
             nc.sync.dma_start(out=gate_sb[:, r, :], in_=gate[r])
 
-        def permute(e):
+        def permute(lo, hi):
             nc.vector.tensor_copy(
-                out=w1_perm[:, e, :].bitcast(U16).rearrange("p (t m) -> p t m", t=4),
-                in_=w1_raw[:, e, :].bitcast(U16).rearrange("p (m t) -> p t m", t=4),
-            )
-            nc.vector.tensor_copy(
-                out=s1_perm[:, e, :].rearrange("p (t m) -> p t m", t=4),
-                in_=s1_raw[:, e, :].rearrange("p (m t) -> p t m", t=4),
+                out=w1_perm[:, lo:hi, :].rearrange("p e b -> p (e b)").bitcast(U16).rearrange("p (e t m) -> p e t m", e=hi - lo, t=4),
+                in_=w1_raw[:, lo:hi, :].rearrange("p e b -> p (e b)").bitcast(U16).rearrange("p (e m t) -> p e t m", e=hi - lo, t=4),
             )
 
         def cast(engine, lo, hi):
@@ -106,11 +107,11 @@ def tile_moe_cap2_mlp_gelu_kernel(tc, xT, w1_words, w1_scales, w2_words, w2_scal
                 in_=x_bf[:, lo:hi, :].rearrange("p t j -> p (t j)"),
             )
 
-        permute(2)
-        permute(3)
+        permute(0, 2)
+        permute(2, 4)
         cast("scalar", 0, 256)
-        cast("vector", 256, 416)
-        cast("scalar", 416, 512)
+        cast("vector", 256, 464)
+        cast("scalar", 464, 512)
         quantize_x(0, 512)
         cast("vector", 512, 672)
         cast("scalar", 672, 768)
@@ -138,7 +139,7 @@ def tile_moe_cap2_mlp_gelu_kernel(tc, xT, w1_words, w1_scales, w2_words, w2_scal
                     nc.tensor.matmul_mx(
                         out=bank[:, t * U : (t + 1) * U],
                         lhsT=w1_perm[:, e, t * 256 : (t + 1) * 256].bitcast(FP4X4),
-                        lhsT_scale=s1_perm[:, e, t * 128 : (t + 1) * 128],
+                        lhsT_scale=s1_planes[e][:, t * 128 : (t + 1) * 128],
                         rhs=g_codes[e][:, cols].bitcast(FP8X4),
                         rhs_scale=g_scales[e][:, cols],
                         start=True,
@@ -163,58 +164,25 @@ def tile_moe_cap2_mlp_gelu_kernel(tc, xT, w1_words, w1_scales, w2_words, w2_scal
                 stop=True,
             )
 
-        def first_layer_moving(e):
-            rows = []
-            for u in range(2):
-                bank = apsum.tile([P, 4 * U], F32, name="bank")
-                cols = slice(u * U, (u + 1) * U)
-                nc.tensor.matmul_mx(
-                    out=bank[:],
-                    lhsT=g_codes[e][:, cols].bitcast(FP8X4),
-                    lhsT_scale=g_scales[e][:, cols],
-                    rhs=w1_raw[:, e, :].bitcast(FP4X4),
-                    rhs_scale=s1_raw[:, e, :],
-                    start=True,
-                    stop=True,
-                )
-                h_rows = keep.tile([P, H], BF16, name="h_rows%d_%d" % (e, u), align_bytes=64)
-                nc.scalar.activation(out=h_rows[:], in_=bank[:], func=ACT.Gelu_apprx_tanh)
-                rows.append(h_rows)
-            return rows
-
-        def turn(e, u, h_rows, engine):
-            words = h_rows[:].bitcast(F32).rearrange("p (w v) -> p v w", v=2)
-            turned = xpsum.tile([P, 2, P], F32, name="turned")
-            for v in range(2):
-                nc.tensor.transpose(turned[:, v, :], words[:, v, :], ident[:])
-            dst = h[e][:, u * U : (u + 1) * U, :].rearrange("p c t -> p (c t)").bitcast(F32).rearrange("p (c v) -> p c v", v=2)
-            src = turned[:].rearrange("p v c -> p c v")
-            if engine == "scalar":
-                nc.scalar.copy(out=dst, in_=src)
-            else:
-                nc.vector.tensor_copy(out=dst, in_=src)
-
         gather(0, 0, U)
         gather(0, U, C)
-        rows0 = first_layer_moving(0)
+        first_layer(0)
         gather(1, 0, C)
-        turn(0, 0, rows0[0], "vector")
-        rows1 = first_layer_moving(1)
-        turn(0, 1, rows0[1], "scalar")
+        first_layer(1)
         gather(2, 0, C)
-        second_layer(0, 0, C)
         first_layer(2)
-        turn(1, 0, rows1[0], "vector")
-        turn(1, 1, rows1[1], "scalar")
-        gather(3, 0, C)
-        second_layer(1, 0, C)
+        second_layer(0, 0, C)
+        gather(3, 0, U)
+        gather(3, U, C)
         first_layer(3)
-        second_layer(2, 0, C)
+        second_layer(1, 0, C)
         nc.scalar.copy(out=y_sb[:, 0 : 2 * C], in_=y_banks[0][:])
+        second_layer(2, 0, C)
         second_layer(3, 0, U)
-        nc.vector.tensor_copy(out=y_sb[:, 2 * C : 3 * C + U], in_=y_banks[1][:, 0 : C + U])
+        nc.vector.tensor_copy(out=y_sb[:, 2 * C : 3 * C], in_=y_banks[1][:, 0:C])
         second_layer(3, U, C)
-        nc.scalar.copy(out=y_sb[:, 3 * C + U : 4 * C], in_=y_banks[1][:, C + U : 2 * C])
+        nc.vector.tensor_copy(out=y_sb[:, 3 * C : 3 * C + U], in_=y_banks[1][:, C : C + U])
+        nc.vector.tensor_copy(out=y_sb[:, 3 * C + U : 4 * C], in_=y_banks[1][:, C + U : 2 * C])
 
         def pick(lo, hi, p_sb, r, t):
             nc.vector.tensor_tensor(t[:, lo:hi], y_sb[:].indirect(p_sb[:, lo // 16 : hi // 16]), gate_sb[:, r, lo:hi], ALU.mult)

@@ -60,16 +60,17 @@ def tile_moe_cap2_mlp_gelu_kernel(tc, xT, w1_words, w1_scales, w2_words, w2_scal
         x_view = xT.rearrange("(p j) t -> p j t", j=4)
         s1_i32 = w1_scales.rearrange("e s q h -> (e s) q h").bitcast(I32)
         s2_i32 = w2_scales.rearrange("e s q h -> q (e s) h").bitcast(I32)
-        for q in range(4):
-            nc.sync.dma_start(out=s1_raw[32 * q : 32 * q + 16, :].bitcast(I32), in_=s1_i32[:, 4 * q : 4 * q + 4, :])
         nc.scalar.activation(out=dummy2[:], in_=dummy[:], func=ACT.Gelu_apprx_tanh)
 
         w1_i32 = w1_words.rearrange("e s p b -> p (e s) b").bitcast(I32)
-        for lo in range(0, E, 2):
-            nc.sync.dma_start(out=w1_raw[:, lo : lo + 2, :].bitcast(I32), in_=w1_i32[:, lo : lo + 2, :])
-        for lo in range(0, T, 256):
-            nc.sync.dma_start(out=x_raw[:, :, lo : lo + 256], in_=x_view[:, :, lo : lo + 256])
+        nc.sync.dma_start(out=w1_raw[:, 0:1, :].bitcast(I32), in_=w1_i32[:, 0:1, :])
+        for q in range(4):
+            nc.sync.dma_start(out=s1_raw[32 * q : 32 * q + 16, :].bitcast(I32), in_=s1_i32[:, 4 * q : 4 * q + 4, :])
+        nc.sync.dma_start(out=w1_raw[:, 1:3, :].bitcast(I32), in_=w1_i32[:, 1:3, :])
+        for lo, hi in ((0, 512), (512, 768)):
+            nc.sync.dma_start(out=x_raw[:, :, lo:hi], in_=x_view[:, :, lo:hi])
         nc.sync.dma_start(offs_sb[:], offs)
+        nc.sync.dma_start(out=w1_raw[:, 3:4, :].bitcast(I32), in_=w1_i32[:, 3:4, :])
 
         nc.vector.tensor_copy(
             out=s1_perm[:].rearrange("p (t m) -> p t m", t=4),
@@ -107,14 +108,14 @@ def tile_moe_cap2_mlp_gelu_kernel(tc, xT, w1_words, w1_scales, w2_words, w2_scal
                 in_=x_bf[:, lo:hi, :].rearrange("p t j -> p (t j)"),
             )
 
-        permute(0, 2)
-        permute(2, 4)
-        cast("scalar", 0, 256)
-        cast("vector", 256, 464)
-        cast("scalar", 464, 512)
-        quantize_x(0, 512)
+        permute(0, 1)
+        permute(1, 3)
+        cast("vector", 0, 256)
+        cast("scalar", 256, 512)
+        quantize_x(0, 256)
         cast("vector", 512, 672)
         cast("scalar", 672, 768)
+        quantize_x(256, 512)
         quantize_x(512, 768)
 
         g_codes = [keep.tile([P, C], U32, name="g_codes%d" % e, align_bytes=64) for e in range(E)]
@@ -169,15 +170,17 @@ def tile_moe_cap2_mlp_gelu_kernel(tc, xT, w1_words, w1_scales, w2_words, w2_scal
         first_layer(0)
         gather(1, 0, C)
         first_layer(1)
+        second_layer(0, 0, C)
+        nc.scalar.copy(out=y_sb[:, 0:C], in_=y_banks[0][:, 0:C])
+        permute(3, 4)
         gather(2, 0, C)
         first_layer(2)
-        second_layer(0, 0, C)
         gather(3, 0, U)
         gather(3, U, C)
         first_layer(3)
         second_layer(1, 0, C)
-        nc.scalar.copy(out=y_sb[:, 0 : 2 * C], in_=y_banks[0][:])
         second_layer(2, 0, C)
+        nc.vector.tensor_copy(out=y_sb[:, C : 2 * C], in_=y_banks[0][:, C : 2 * C])
         second_layer(3, 0, U)
         nc.vector.tensor_copy(out=y_sb[:, 2 * C : 3 * C], in_=y_banks[1][:, 0:C])
         second_layer(3, U, C)
@@ -192,9 +195,7 @@ def tile_moe_cap2_mlp_gelu_kernel(tc, xT, w1_words, w1_scales, w2_words, w2_scal
             nc.sync.dma_start(out=out[:, lo:hi], in_=o_sb[:, lo:hi])
 
         pick(0, 768, pos1_sb, 0, t1)
-        pick(0, 384, pos2_sb, 1, t2)
-        pick(384, 640, pos2_sb, 1, t2)
-        finish(0, 384)
-        pick(640, 768, pos2_sb, 1, t2)
-        finish(384, 640)
-        finish(640, 768)
+        pick(0, 512, pos2_sb, 1, t2)
+        pick(512, 768, pos2_sb, 1, t2)
+        finish(0, 512)
+        finish(512, 768)

@@ -126,6 +126,7 @@ def tile_moe_cap2_mlp_gelu_kernel(tc, xT, w1_words, w1_scales, w2_words, w2_scal
             nc.vector.tensor_copy(g_codes[e][:, lo:hi], x_codes[:].indirect(lst))
             nc.vector.tensor_copy(g_scales[e][:, lo:hi], x_scales[:].indirect(lst))
 
+        y_place = ((0, 0), (1, 0), (1, C), (0, C))
         y_banks = [ypsum.tile([P, 2 * C], F32, name="y_bank%d" % b) for b in range(2)]
 
         h = [keep.tile([P, C, 4], BF16, name="h%d" % e, align_bytes=64) for e in range(E)]
@@ -154,9 +155,9 @@ def tile_moe_cap2_mlp_gelu_kernel(tc, xT, w1_words, w1_scales, w2_words, w2_scal
                 scales=h_scales[e][:, lo:hi],
                 in_=h[e][:, lo:hi, :].rearrange("p c t -> p (c t)"),
             )
-            base = (e % 2) * C
+            bank, base = y_place[e]
             nc.tensor.matmul_mx(
-                out=y_banks[e // 2][:, base + lo : base + hi],
+                out=y_banks[bank][:, base + lo : base + hi],
                 lhsT=w2_sb[:, e, :].bitcast(FP4X4),
                 lhsT_scale=s2_sb[:, e, :],
                 rhs=h_codes[e][:, lo:hi].bitcast(FP8X4),
@@ -180,12 +181,10 @@ def tile_moe_cap2_mlp_gelu_kernel(tc, xT, w1_words, w1_scales, w2_words, w2_scal
         first_layer(3)
         second_layer(1, 0, C)
         second_layer(2, 0, C)
-        nc.vector.tensor_copy(out=y_sb[:, C : 2 * C], in_=y_banks[0][:, C : 2 * C])
         second_layer(3, 0, U)
-        nc.vector.tensor_copy(out=y_sb[:, 2 * C : 3 * C], in_=y_banks[1][:, 0:C])
+        nc.scalar.copy(out=y_sb[:, C : 3 * C], in_=y_banks[1][:])
         second_layer(3, U, C)
-        nc.vector.tensor_copy(out=y_sb[:, 3 * C : 3 * C + U], in_=y_banks[1][:, C : C + U])
-        nc.vector.tensor_copy(out=y_sb[:, 3 * C + U : 4 * C], in_=y_banks[1][:, C + U : 2 * C])
+        nc.vector.tensor_copy(out=y_sb[:, 3 * C : 4 * C], in_=y_banks[0][:, C : 2 * C])
 
         def pick(lo, hi, p_sb, r, t):
             nc.vector.tensor_tensor(t[:, lo:hi], y_sb[:].indirect(p_sb[:, lo // 16 : hi // 16]), gate_sb[:, r, lo:hi], ALU.mult)

from contextlib import ExitStack

import concourse.mybir as mybir

K, T, E, C, H, N = 512, 768, 4, 256, 512, 128
PAD = 32
S = E * C
P = 128
U = 128

F32 = mybir.dt.float32
BF16 = mybir.dt.bfloat16
I32 = mybir.dt.int32
U32 = mybir.dt.uint32
U16 = mybir.dt.uint16
U8 = mybir.dt.uint8
FP8X4 = mybir.dt.float8_e4m3fn_x4
FP4X4 = mybir.dt.float4_e2m1fn_x4
ACT = mybir.ActivationFunctionType
ALU = mybir.AluOpType

FLOPS = 2 * S * (K * H + H * N)


def tile_moe_cap2_mlp_gelu_kernel(tc, xT, w1_words, w1_scales, w2_words, w2_scales, gate, offs, pos1, pos2, out):
    nc = tc.nc
    with ExitStack() as ctx:
        keep = ctx.enter_context(tc.tile_pool(name="keep", bufs=1))
        apsum = ctx.enter_context(tc.psum_pool(name="apsum", bufs=6))
        ypsum = ctx.enter_context(tc.psum_pool(name="ypsum", bufs=1))

        offs_sb = keep.tile([P, S // 16], U16, name="offs_sb")
        pos1_sb = keep.tile([P, T // 16], U16, name="pos1_sb")
        pos2_sb = keep.tile([P, T // 16], U16, name="pos2_sb")
        x_raw = keep.tile([P, 4, T], F32, name="x_raw")
        x_bf = keep.tile([P, T, 4], BF16, name="x_bf", align_bytes=64)
        x_codes = keep.tile([P, T], U32, name="x_codes", align_bytes=64)
        x_scales = keep.tile([P, T], U8, name="x_scales", align_bytes=64)
        w1_raw = keep.tile([P, E, 2 * H], U8, name="w1_raw", align_bytes=64)
        w1_perm = keep.tile([P, E, 2 * H], U8, name="w1_perm", align_bytes=64)
        s1_raw = keep.tile([P, H], U8, name="s1_raw", align_bytes=64)
        s1_perm = keep.tile([P, H], U8, name="s1_perm", align_bytes=64)
        s1_planes = [s1_perm] + [keep.tile([P, H], U8, name="s1_plane%d" % e, align_bytes=64) for e in range(1, E)]
        w2_sb = keep.tile([P, E, 2 * N], U8, name="w2_sb", align_bytes=64)
        s2_sb = keep.tile([P, E, N], U8, name="s2_sb", align_bytes=64)
        gate_sb = keep.tile([P, 2, T], F32, name="gate_sb")
        y_sb = keep.tile([P, S + PAD], F32, name="y_sb")
        t1 = keep.tile([P, T], F32, name="t1")
        t2 = keep.tile([P, T], F32, name="t2")
        o_sb = keep.tile([P, T], F32, name="o_sb")
        dummy = keep.tile([P, 1], F32, name="dummy")
        dummy2 = keep.tile([P, 1], F32, name="dummy2")

        nc.vector.memset(s1_raw[:].bitcast(I32), 0)
        nc.vector.memset(dummy[:], 0.0)
        nc.vector.memset(x_scales[:].bitcast(I32), 0)
        nc.vector.memset(s2_sb[:].rearrange("p e h -> p (e h)").bitcast(I32), 0)
        nc.vector.memset(y_sb[:, S : S + PAD], 0.0)

        x_view = xT.rearrange("(p j) t -> p j t", j=4)
        s1_i32 = w1_scales.rearrange("e s q h -> (e s) q h").bitcast(I32)
        s2_i32 = w2_scales.rearrange("e s q h -> q (e s) h").bitcast(I32)
        nc.scalar.activation(out=dummy2[:], in_=dummy[:], func=ACT.Gelu_apprx_tanh)

        w1_i32 = w1_words.rearrange("e s p b -> p (e s) b").bitcast(I32)
        nc.sync.dma_start(out=w1_raw[:, 0:1, :].bitcast(I32), in_=w1_i32[:, 0:1, :])
        for q in range(4):
            nc.sync.dma_start(out=s1_raw[32 * q : 32 * q + 16, :].bitcast(I32), in_=s1_i32[:, 4 * q : 4 * q + 4, :])
        nc.sync.dma_start(out=w1_raw[:, 1:3, :].bitcast(I32), in_=w1_i32[:, 1:3, :])
        for lo, hi in ((0, 512), (512, 768)):
            nc.sync.dma_start(out=x_raw[:, :, lo:hi], in_=x_view[:, :, lo:hi])
        nc.sync.dma_start(offs_sb[:], offs)
        nc.sync.dma_start(out=w1_raw[:, 3:4, :].bitcast(I32), in_=w1_i32[:, 3:4, :])

        nc.vector.tensor_copy(
            out=s1_perm[:].rearrange("p (t m) -> p t m", t=4),
            in_=s1_raw[:].rearrange("p (m t) -> p t m", t=4),
        )
        for e in range(1, E):
            rows = P - 4 * e
            nc.sync.dma_start(out=s1_planes[e][0:rows, :].bitcast(I32), in_=s1_perm[4 * e : P, :].bitcast(I32))
        nc.sync.dma_start(out=w2_sb[:].bitcast(I32), in_=w2_words.rearrange("e s p b -> p (e s) b").bitcast(I32))
        for q in range(4):
            nc.sync.dma_start(out=s2_sb[32 * q : 32 * q + 4, :, :].bitcast(I32), in_=s2_i32[4 * q : 4 * q + 4, :, :])
        nc.sync.dma_start(pos1_sb[:], pos1)
        nc.sync.dma_start(pos2_sb[:], pos2)
        for r in range(2):
            nc.sync.dma_start(out=gate_sb[:, r, :], in_=gate[r])

        def permute(lo, hi):
            nc.vector.tensor_copy(
                out=w1_perm[:, lo:hi, :].rearrange("p e b -> p (e b)").bitcast(U16).rearrange("p (e t m) -> p e t m", e=hi - lo, t=4),
                in_=w1_raw[:, lo:hi, :].rearrange("p e b -> p (e b)").bitcast(U16).rearrange("p (e m t) -> p e t m", e=hi - lo, t=4),
            )

        def cast(engine, lo, hi):
            dst = x_bf[:, lo:hi, :].rearrange("p (c i) j -> p c j i", i=4)
            src = x_raw[:, :, lo:hi].rearrange("p j (c i) -> p c j i", i=4)
            if engine == "scalar":
                nc.scalar.copy(out=dst, in_=src)
            else:
                nc.vector.tensor_copy(out=dst, in_=src)

        def quantize_x(lo, hi):
            nc.vector.quantize_mx(
                out=x_codes[:, lo:hi].bitcast(FP8X4),
                scales=x_scales[:, lo:hi],
                in_=x_bf[:, lo:hi, :].rearrange("p t j -> p (t j)"),
            )

        permute(0, 1)
        permute(1, 3)
        cast("vector", 0, 256)
        cast("scalar", 256, 512)
        quantize_x(0, 256)
        cast("vector", 512, 672)
        cast("scalar", 672, 768)
        quantize_x(256, 512)
        quantize_x(512, 768)

        g_codes = [keep.tile([P, C], U32, name="g_codes%d" % e, align_bytes=64) for e in range(E)]
        g_scales = [keep.tile([P, C], U8, name="g_scales%d" % e, align_bytes=64) for e in range(E)]

        def gather(e, lo, hi):
            lst = offs_sb[:, (e * C + lo) // 16 : (e * C + hi) // 16]
            nc.vector.tensor_copy(g_codes[e][:, lo:hi], x_codes[:].indirect(lst))
            nc.vector.tensor_copy(g_scales[e][:, lo:hi], x_scales[:].indirect(lst))

        y_place = ((0, 0), (1, 0), (1, C), (0, C))
        y_banks = [ypsum.tile([P, 2 * C], F32, name="y_bank%d" % b) for b in range(2)]

        h = [keep.tile([P, C, 4], BF16, name="h%d" % e, align_bytes=64) for e in range(E)]
        h_codes = [keep.tile([P, C], U32, name="h_codes%d" % e, align_bytes=64) for e in range(E)]
        h_scales = [keep.tile([P, C], U8, name="h_scales%d" % e, align_bytes=64) for e in range(E)]

        def first_layer(e):
            for u in range(2):
                bank = apsum.tile([P, 4 * U], F32, name="bank")
                cols = slice(u * U, (u + 1) * U)
                for t in range(4):
                    nc.tensor.matmul_mx(
                        out=bank[:, t * U : (t + 1) * U],
                        lhsT=w1_perm[:, e, t * 256 : (t + 1) * 256].bitcast(FP4X4),
                        lhsT_scale=s1_planes[e][:, t * 128 : (t + 1) * 128],
                        rhs=g_codes[e][:, cols].bitcast(FP8X4),
                        rhs_scale=g_scales[e][:, cols],
                        start=True,
                        stop=True,
                    )
                nc.scalar.activation(out=h[e][:, cols, :], in_=bank[:].rearrange("p (t c) -> p c t", t=4), func=ACT.Gelu_apprx_tanh)

        def second_layer(e, lo, hi):
            nc.vector.quantize_mx(
                out=h_codes[e][:, lo:hi].bitcast(FP8X4),
                scales=h_scales[e][:, lo:hi],
                in_=h[e][:, lo:hi, :].rearrange("p c t -> p (c t)"),
            )
            bank, base = y_place[e]
            nc.tensor.matmul_mx(
                out=y_banks[bank][:, base + lo : base + hi],
                lhsT=w2_sb[:, e, :].bitcast(FP4X4),
                lhsT_scale=s2_sb[:, e, :],
                rhs=h_codes[e][:, lo:hi].bitcast(FP8X4),
                rhs_scale=h_scales[e][:, lo:hi],
                start=True,
                stop=True,
            )

        gather(0, 0, U)
        gather(0, U, C)
        first_layer(0)
        gather(1, 0, C)
        first_layer(1)
        second_layer(0, 0, C)
        nc.scalar.copy(out=y_sb[:, 0:C], in_=y_banks[0][:, 0:C])
        permute(3, 4)
        gather(2, 0, C)
        first_layer(2)
        gather(3, 0, U)
        gather(3, U, C)
        first_layer(3)
        second_layer(1, 0, C)
        second_layer(2, 0, C)
        second_layer(3, 0, U)
        nc.scalar.copy(out=y_sb[:, C : 3 * C], in_=y_banks[1][:])
        second_layer(3, U, C)
        nc.vector.tensor_copy(out=y_sb[:, 3 * C : 4 * C], in_=y_banks[0][:, C : 2 * C])

        def pick(lo, hi, p_sb, r, t):
            nc.vector.tensor_tensor(t[:, lo:hi], y_sb[:].indirect(p_sb[:, lo // 16 : hi // 16]), gate_sb[:, r, lo:hi], ALU.mult)

        def finish(lo, hi):
            nc.vector.tensor_add(o_sb[:, lo:hi], t1[:, lo:hi], t2[:, lo:hi])
            nc.sync.dma_start(out=out[:, lo:hi], in_=o_sb[:, lo:hi])

        pick(0, 768, pos1_sb, 0, t1)
        pick(0, 512, pos2_sb, 1, t2)
        pick(512, 768, pos2_sb, 1, t2)
        finish(0, 512)
        finish(512, 768)
